import numpy as np
import ml_dtypes


def mxq(x, axis, fmt="e4m3"):
    dtype, down = {"e4m3": (ml_dtypes.float8_e4m3fn, 7), "e5m2": (ml_dtypes.float8_e5m2, 14)}[fmt]
    v = np.moveaxis(np.asarray(x, np.float32).astype(ml_dtypes.bfloat16).astype(np.float64), axis, -1)
    blocks = v.reshape(v.shape[:-1] + (-1, 32))
    amax = np.abs(blocks).max(-1, keepdims=True)
    byte = np.maximum(np.where(amax > 0, np.frexp(amax)[1] - 1 + 127, 0) - down, 1)
    scale = np.exp2(byte - 127.0)
    codes = (blocks / scale).astype(np.float32).astype(dtype).astype(np.float64)
    return np.moveaxis((codes * scale).reshape(v.shape), -1, axis)


WIDE = False


def mx_kscale(k):
    if not WIDE:
        return np.ones(k)
    levels = np.array([10, -10, 5, -5, 0])
    if k % 512:
        return np.exp2(np.random.permutation(np.resize(levels, k // 32))).repeat(32)
    a = np.empty((k // 512, 16))
    for p in range(k // 512):
        a[p, :8] = np.random.permutation(np.resize(levels, 8))
        for g in range(8):
            far = levels[np.abs(levels - a[p, g]) >= 10]
            a[p, g + 8] = far[np.random.randint(len(far))]
    return np.exp2(a.ravel()).repeat(32)


BF16 = ml_dtypes.bfloat16


def bf(x):
    return np.asarray(x, np.float32).astype(BF16)


def f64(x):
    return np.asarray(x).astype(np.float64)


E2M1 = np.array([0.0, 0.5, 1.0, 1.5, 2.0, 3.0, 4.0, 6.0, -0.0, -0.5, -1.0, -1.5, -2.0, -3.0, -4.0, -6.0])


def pack_weight(w, fmt):
    k, n = w.shape
    w = f64(bf(w)).reshape(k // 32, 32, n)
    amax = np.abs(w).max(1)
    if fmt == "e4m3":
        byte = np.frexp(amax)[1] - 1 + 127 - 7
    else:
        mant, ex = np.frexp(amax / 6.0)
        byte = np.where(mant > 0.5, ex, ex - 1) + 127
    byte = np.clip(np.where(amax > 0, byte, 1), 1, 254)
    scaled = (w * np.exp2(127.0 - byte)[:, None, :]).reshape(k, n).astype(np.float32)
    by_word = np.ascontiguousarray(scaled.reshape(k // 512, 128, 4, n).transpose(0, 1, 3, 2))
    if fmt == "e4m3":
        words = by_word.astype(ml_dtypes.float8_e4m3fn).view(np.uint8)
    else:
        c = by_word.astype(ml_dtypes.float4_e2m1fn).view(np.uint8) & 0xF
        words = c[..., 0::2] | (c[..., 1::2] << 4)
    return np.ascontiguousarray(words), np.ascontiguousarray(byte.astype(np.uint8).reshape(k // 512, 16, n))


def unpack_weight(words, scales, fmt):
    g, p, n, _ = words.shape
    if fmt == "e4m3":
        vals = np.ascontiguousarray(words).view(ml_dtypes.float8_e4m3fn).astype(np.float64)
    else:
        nib = np.empty((g, p, n, 4), np.uint8)
        nib[..., 0::2] = words & 0xF
        nib[..., 1::2] = words >> 4
        vals = E2M1[nib]
    vals = vals * np.repeat(np.exp2(scales.astype(np.float64) - 127.0), 8, axis=1)[..., None]
    return vals.transpose(0, 1, 3, 2).reshape(g * 512, n)
def pack4(w):
    words, scales = pack_weight(w, "e2m1")
    return words.reshape(words.shape[0], 128, -1), scales


def unpack4(words, scales):
    return unpack_weight(words.reshape(words.shape[0], 128, -1, 2), scales, "e2m1")


Z, S, N, M, R = 4, 1024, 1024, 512, 512


def setup_inputs():
    s, t = mx_kscale(Z * N), mx_kscale(Z * M)
    s3, t3 = s.reshape(Z, 1, N), t.reshape(Z, 1, M)
    mood = 0.4 + 1.2 * np.random.random_sample((Z, S, 1))
    pay = np.random.standard_exponential((Z, S, N)) * mood
    a = np.random.standard_exponential((Z, N, M)) ** 3 / (6 * N)
    b = np.random.standard_exponential((Z, M, R)) ** 3 / (6 * M)
    a_words, a_scales = pack4((a * t3).reshape(Z * N, M) / s[:, None])
    b_words, b_scales = pack4(b.reshape(Z * M, R) / t[:, None])
    cash1 = 0.5 * np.random.standard_exponential((Z, S, M))
    cash2 = 0.5 * np.random.standard_exponential((Z, S, R))
    owed1 = 1.0 + np.random.random_sample((Z, M))
    owed2 = 1.2 + 1.2 * np.random.random_sample((Z, R))
    return {"pay": bf(pay * s3),
            "a_words": a_words, "a_scales": a_scales,
            "b_words": b_words, "b_scales": b_scales,
            "cash1": bf(cash1 * t3), "owed1": bf(owed1 * t.reshape(Z, M)),
            "cash2": bf(cash2), "owed2": bf(owed2)}


def reference(pay, a_words, a_scales, b_words, b_scales, cash1, owed1, cash2, owed2):
    a = unpack4(a_words, a_scales).reshape(Z, N, M)
    b = unpack4(b_words, b_scales).reshape(Z, M, R)
    in1 = mxq(f64(pay), 2, "e4m3") @ a
    paid1 = np.minimum(in1 + f64(cash1), f64(owed1)[:, None, :])
    in2 = mxq(paid1, 2, "e4m3") @ b
    paid2 = np.minimum(in2 + f64(cash2), f64(owed2)[:, None, :])
    return paid2

@@ -1,0 +1,280 @@
+from contextlib import ExitStack
+
+import concourse.mybir as mybir
+from concourse.masks import make_identity
+
+Z, S, N, M, R = 4, 1024, 1024, 512, 512
+FLOPS = 2 * Z * S * (N * M + M * R)
+
+F32 = mybir.dt.float32
+BF16 = mybir.dt.bfloat16
+I32 = mybir.dt.int32
+U32 = mybir.dt.uint32
+U8 = mybir.dt.uint8
+FP8X4 = mybir.dt.float8_e4m3fn_x4
+FP4X4 = mybir.dt.float4_e2m1fn_x4
+ADD = mybir.AluOpType.add
+MIN = mybir.AluOpType.min
+
+P = 128
+PAIR = 2 * P
+PAIRS = Z * S // PAIR
+PER_ZONE = S // PAIR
+LEAD = 5
+DIRECT = 2
+OUT_BUFS = 6
+
+
+def tile_zoned_interbank_clearing_s14_kernel(
+    tc, pay, a_words, a_scales, b_words, b_scales, cash1, owed1, cash2, owed2, out
+):
+    nc = tc.nc
+
+    def rows(t, n):
+        z, q = divmod(n, PER_ZONE)
+        return t[z, q * PAIR : (q + 1) * PAIR, :].rearrange("(p j) k -> p j k", j=2)
+
+    with ExitStack() as ctx:
+        sb = ctx.enter_context(tc.tile_pool(name="sb", bufs=1))
+        ps = ctx.enter_context(tc.psum_pool(name="ps", bufs=1))
+        ctx.enter_context(tc.manual_schedule())
+
+        def ring(name, count, shape, dtype):
+            return [sb.tile(shape, dtype, name="%s%d" % (name, i), align_bytes=64) for i in range(count)]
+
+        ident = sb.tile([P, P], F32)
+        pay_t = [ring("pay%d_" % n, 2, [P, N], BF16) for n in range(PAIRS)]
+        cash1_t = ring("cash1_", PAIRS, [P, 2 * M], BF16)
+        cash2_t = ring("cash2_", PAIRS, [P, 2 * R], BF16)
+        a_t = ring("a", Z, [P, 2, 2 * M], U8)
+        b_t = ring("b", Z, [P, 2 * R], U8)
+        a_sc = sb.tile([P, 2 * Z, M], U8, align_bytes=64)
+        b_sc = sb.tile([P, Z, R], U8, align_bytes=64)
+        owed1_t = sb.tile([P, Z, 4], BF16)
+        owed2_t = sb.tile([P, Z, 4], BF16)
+        owed2_f = sb.tile([P, Z * 4], F32)
+        stage = ring("stage", 2, [P, 1024], F32)
+        pay_codes = ring("pay_codes", 2, [P, 512], U32)
+        pay_sc = ring("pay_sc", 2, [P, 512], U8)
+        paid_codes = ring("paid_codes", 2, [P, 256], U32)
+        paid_sc = ring("paid_sc", 2, [P, 256], U8)
+        have1 = ring("have1_", 2, [P, M], BF16)
+        shared = ring("shared", 3, [P, 1024], F32)
+        in2_sb = ring("in2_sb", 2, [P, 1024], F32)
+        out_t = ring("out_t", OUT_BUFS, [P, 1024], F32)
+
+        payT_ps = [ps.tile([P, 512], F32, name="payT%d" % j) for j in range(2)]
+        in1_ps = [ps.tile([P, 512], F32, name="in1_%d" % j) for j in range(2)]
+        in2_ps = [ps.tile([P, 512], F32, name="in2_%d" % j) for j in range(2)]
+        haveT_ps = ps.tile([P, 512], F32)
+        owed2_ps = ps.tile([P, 512], F32)
+
+        def load_pay(n):
+            for j in range(2):
+                nc.sync.dma_start(out=pay_t[n][j][:], in_=rows(pay, n)[:, j, :])
+
+        def load_cash(dst, src, n):
+            nc.sync.dma_start(out=dst[n][:].rearrange("p (j k) -> p j k", j=2), in_=rows(src, n))
+
+        def load_scales(dst, src):
+            for q in range(4):
+                nc.sync.dma_start(
+                    out=dst[32 * q : 32 * q + 4, :, :].bitcast(I32),
+                    in_=src.bitcast(I32)[:, 4 * q : 4 * q + 4, :].rearrange("g r n -> r g n"),
+                )
+
+        def load_a(z):
+            nc.sync.dma_start(
+                out=a_t[z][:].bitcast(I32),
+                in_=a_words.bitcast(I32)[2 * z : 2 * z + 2, :, :].rearrange("g p n -> p g n"),
+            )
+
+        def load_b(z):
+            nc.sync.dma_start(out=b_t[z][:].bitcast(I32), in_=b_words.bitcast(I32)[z, :, :])
+
+        def load_owed(dst, src):
+            nc.sync.dma_start(out=dst[:], in_=src.rearrange("z (p t) -> p z t", t=4))
+
+        def loads_needed_in(period):
+            n = period + 3
+            if 0 <= n < PAIRS:
+                load_pay(n)
+            n = period + 2
+            if n == 0:
+                load_scales(a_sc, a_scales)
+            if 0 <= n < PAIRS and n % PER_ZONE == 0:
+                load_a(n // PER_ZONE)
+            if 0 <= n < PAIRS:
+                load_cash(cash1_t, cash1, n)
+            if period == -1:
+                load_owed(owed1_t, owed1)
+                load_scales(b_sc, b_scales)
+            if 0 <= period < PAIRS and period % PER_ZONE == 0:
+                load_b(period // PER_ZONE)
+            if period == 0:
+                load_owed(owed2_t, owed2)
+            n = period - 1
+            if 0 <= n < PAIRS:
+                load_cash(cash2_t, cash2, n)
+
+        def transpose_pay(n, j, g):
+            words = pay_t[n][j][:].bitcast(F32)
+            for u in range(2):
+                c = (2 * g + u) * P
+                nc.tensor.transpose(
+                    payT_ps[j][:, c : c + P], words[:, 256 * g + u : 256 * (g + 1) : 2], ident[:]
+                )
+
+        def copy_payT(n, j):
+            nc.scalar.copy(
+                out=stage[n % 2][:, 512 * j : 512 * (j + 1)].rearrange("p (g s u) -> p g s u", g=2, u=2),
+                in_=payT_ps[j][:].rearrange("p (g u s) -> p g s u", g=2, u=2),
+            )
+
+        def quantize_pay(n):
+            nc.vector.quantize_mx(
+                out=pay_codes[n % 2][:].bitcast(FP8X4), scales=pay_sc[n % 2][:], in_=stage[n % 2][:].bitcast(BF16)
+            )
+
+        def matmul1(n, j, g):
+            z = n // PER_ZONE
+            cols = slice((2 * j + g) * P, (2 * j + g + 1) * P)
+            nc.tensor.matmul_mx(
+                out=in1_ps[j][:],
+                lhsT=pay_codes[n % 2][:, cols].bitcast(FP8X4),
+                lhsT_scale=pay_sc[n % 2][:, cols],
+                rhs=a_t[z][:, g, :].bitcast(FP4X4),
+                rhs_scale=a_sc[:, 2 * z + g, :],
+                start=(g == 0),
+                stop=(g == 1),
+            )
+
+        def add_cash1(n, j):
+            nc.vector.tensor_tensor(
+                out=have1[j][:].rearrange("s (u p e) -> s u p e", u=2, e=2),
+                in0=in1_ps[j][:].rearrange("s (p u e) -> s u p e", u=2, e=2),
+                in1=cash1_t[n][:, M * j : M * (j + 1)].rearrange("s (p u e) -> s u p e", u=2, e=2),
+                op=ADD,
+            )
+
+        def transpose_have(j):
+            words = have1[j][:].bitcast(F32)
+            for u in range(2):
+                c = (2 * u + j) * P
+                nc.tensor.transpose(haveT_ps[:, c : c + P], words[:, u * P : (u + 1) * P], ident[:])
+
+        def paid_view(n):
+            return shared[n % 3][:, 0:512].bitcast(BF16)
+
+        def min_owed1(n):
+            z = n // PER_ZONE
+            nc.vector.tensor_tensor(
+                out=paid_view(n).rearrange("p (s u e) -> p s u e", u=2, e=2),
+                in0=haveT_ps[:].bitcast(BF16).rearrange("p (u s e) -> p s u e", u=2, e=2),
+                in1=owed1_t[:, z, :].rearrange("p (u e) -> p u e", e=2).unsqueeze(1).to_broadcast([P, PAIR, 2, 2]),
+                op=MIN,
+            )
+
+        def quantize_paid(n):
+            nc.vector.quantize_mx(out=paid_codes[n % 2][:].bitcast(FP8X4), scales=paid_sc[n % 2][:], in_=paid_view(n))
+
+        def matmul2(n, j):
+            z = n // PER_ZONE
+            cols = slice(j * P, (j + 1) * P)
+            nc.tensor.matmul_mx(
+                out=in2_ps[j][:],
+                lhsT=paid_codes[n % 2][:, cols].bitcast(FP8X4),
+                lhsT_scale=paid_sc[n % 2][:, cols],
+                rhs=b_t[z][:].bitcast(FP4X4),
+                rhs_scale=b_sc[:, z, :],
+                start=True,
+                stop=True,
+            )
+
+        def copy_in2(n, j):
+            nc.scalar.copy(out=in2_sb[n % 2][:, R * j : R * (j + 1)], in_=in2_ps[j][:])
+
+        def add_cash2_gpsimd(n):
+            nc.gpsimd.tensor_tensor(out=shared[(n + 1) % 3][:], in0=in2_sb[n % 2][:], in1=cash2_t[n][:], op=ADD)
+
+        def add_cash2_vector(n, j):
+            cols = slice(R * j, R * (j + 1))
+            nc.vector.tensor_tensor(out=in2_sb[n % 2][:, cols], in0=in2_ps[j][:], in1=cash2_t[n][:, cols], op=ADD)
+
+        def spread_owed2(z):
+            for t in range(4):
+                c = 4 * z + t
+                nc.tensor.transpose(owed2_ps[:, t:R:4], owed2_f[:, c : c + 1].to_broadcast([P, P]), ident[:])
+
+        def min_owed2_pair(n):
+            nc.vector.tensor_tensor(
+                out=out_t[n % OUT_BUFS][:].rearrange("s (j r) -> s j r", j=2),
+                in0=shared[(n + 1) % 3][:].rearrange("s (j r) -> s j r", j=2),
+                in1=owed2_ps[:].unsqueeze(1).to_broadcast([P, 2, R]),
+                op=MIN,
+            )
+            nc.sync.dma_start(out=rows(out, n), in_=out_t[n % OUT_BUFS][:].rearrange("s (j r) -> s j r", j=2))
+
+        def min_owed2_tile(n, j):
+            cols = slice(R * j, R * (j + 1))
+            nc.vector.tensor_tensor(out=out_t[n % OUT_BUFS][:, cols], in0=in2_sb[n % 2][:, cols], in1=owed2_ps[:], op=MIN)
+            nc.sync.dma_start(out=rows(out, n)[:, j, :], in_=out_t[n % OUT_BUFS][:, cols])
+
+        def live(n, upto=PAIRS):
+            return 0 <= n < upto
+
+        via_gpsimd = PAIRS - DIRECT
+
+        nc.vector.memset(a_sc[:].rearrange("p g n -> p (g n)").bitcast(I32), 0)
+        nc.vector.memset(b_sc[:].rearrange("p g n -> p (g n)").bitcast(I32), 0)
+        make_identity(nc, ident[:])
+        for period in range(-3, -3 + LEAD):
+            loads_needed_in(period)
+
+        for w in range(-3, PAIRS):
+            loads_needed_in(w + LEAD)
+            if live(w + 2):
+                quantize_pay(w + 2)
+            if live(w):
+                quantize_paid(w)
+            if live(w - 1, via_gpsimd):
+                add_cash2_gpsimd(w - 1)
+            if live(w + 3):
+                transpose_pay(w + 3, 0, 0)
+            if live(w + 1):
+                transpose_have(1)
+                min_owed1(w + 1)
+            if w == 0:
+                nc.scalar.copy(out=owed2_f[:], in_=owed2_t[:].rearrange("p z t -> p (z t)"))
+            if live(w - 2) and (w - 2) % PER_ZONE == 0:
+                spread_owed2((w - 2) // PER_ZONE)
+            if live(w + 3):
+                transpose_pay(w + 3, 0, 1)
+                copy_payT(w + 3, 0)
+            if live(w + 2):
+                matmul1(w + 2, 0, 0)
+                matmul1(w + 2, 0, 1)
+                matmul1(w + 2, 1, 0)
+            if live(w + 3):
+                transpose_pay(w + 3, 1, 0)
+                transpose_pay(w + 3, 1, 1)
+                copy_payT(w + 3, 1)
+            if live(w + 2):
+                matmul1(w + 2, 1, 1)
+            if live(w):
+                matmul2(w, 0)
+                matmul2(w, 1)
+            if live(w, via_gpsimd):
+                copy_in2(w, 0)
+                copy_in2(w, 1)
+            if live(w - 2, via_gpsimd):
+                min_owed2_pair(w - 2)
+            if live(w + 2):
+                add_cash1(w + 2, 0)
+                add_cash1(w + 2, 1)
+                transpose_have(0)
+            if live(w) and w >= via_gpsimd:
+                add_cash2_vector(w, 0)
+                add_cash2_vector(w, 1)
+                min_owed2_tile(w, 0)
+                min_owed2_tile(w, 1)

@@ -21,8 +21,9 @@ PAIR = 2 * P
 PAIRS = Z * S // PAIR
 PER_ZONE = S // PAIR
 LEAD = 5
-DIRECT = 2
 OUT_BUFS = 6
+SORTED_TILES = (1,)
+FIRST_G = 0
 
 
 def tile_zoned_interbank_clearing_s14_kernel(
@@ -43,23 +44,25 @@ def tile_zoned_interbank_clearing_s14_kernel(
             return [sb.tile(shape, dtype, name="%s%d" % (name, i), align_bytes=64) for i in range(count)]
 
         ident = sb.tile([P, P], F32)
-        pay_t = [ring("pay%d_" % n, 2, [P, N], BF16) for n in range(PAIRS)]
+        pay_t = ring("pay", PAIRS, [P, 2 * N], BF16)
+        sorted_t = ring("sorted", 2, [P, 512], F32)
         cash1_t = ring("cash1_", PAIRS, [P, 2 * M], BF16)
         cash2_t = ring("cash2_", PAIRS, [P, 2 * R], BF16)
         a_t = ring("a", Z, [P, 2, 2 * M], U8)
         b_t = ring("b", Z, [P, 2 * R], U8)
-        a_sc = sb.tile([P, 2 * Z, M], U8, align_bytes=64)
+        a_sc_first = sb.tile([P, 2, M], U8, align_bytes=64)
+        a_sc_rest = sb.tile([P, 2 * (Z - 1), M], U8, align_bytes=64)
         b_sc = sb.tile([P, Z, R], U8, align_bytes=64)
-        owed1_t = sb.tile([P, Z, 4], BF16)
-        owed2_t = sb.tile([P, Z, 4], BF16)
-        owed2_f = sb.tile([P, Z * 4], F32)
-        stage = ring("stage", 2, [P, 1024], F32)
+        a_sc = [a_sc_first[:, g, :] for g in range(2)] + [a_sc_rest[:, g, :] for g in range(2 * (Z - 1))]
+        owed_rows = sb.tile([P, M], BF16)
+        owed_t = sb.tile([P, 2 * Z, 4], BF16)
+        stage = ring("stage", 3, [P, 1024], F32)
         pay_codes = ring("pay_codes", 2, [P, 512], U32)
         pay_sc = ring("pay_sc", 2, [P, 512], U8)
         paid_codes = ring("paid_codes", 2, [P, 256], U32)
         paid_sc = ring("paid_sc", 2, [P, 256], U8)
         have1 = ring("have1_", 2, [P, M], BF16)
-        shared = ring("shared", 3, [P, 1024], F32)
+        paid_t = ring("paid", 2, [P, 1024], F32)
         in2_sb = ring("in2_sb", 2, [P, 1024], F32)
         out_t = ring("out_t", OUT_BUFS, [P, 1024], F32)
 
@@ -68,19 +71,23 @@ def tile_zoned_interbank_clearing_s14_kernel(
         in2_ps = [ps.tile([P, 512], F32, name="in2_%d" % j) for j in range(2)]
         haveT_ps = ps.tile([P, 512], F32)
         owed2_ps = ps.tile([P, 512], F32)
+        owed2_row = owed2_ps[:, 0:256].bitcast(BF16)
 
         def load_pay(n):
-            for j in range(2):
-                nc.sync.dma_start(out=pay_t[n][j][:], in_=rows(pay, n)[:, j, :])
+            if n < 2:
+                for j in range(2):
+                    nc.sync.dma_start(out=pay_t[n][:, N * j : N * (j + 1)], in_=rows(pay, n)[:, j, :])
+            else:
+                nc.sync.dma_start(out=pay_t[n][:].rearrange("p (j k) -> p j k", j=2), in_=rows(pay, n))
 
         def load_cash(dst, src, n):
             nc.sync.dma_start(out=dst[n][:].rearrange("p (j k) -> p j k", j=2), in_=rows(src, n))
 
-        def load_scales(dst, src):
+        def load_scales(dst, src, g0, g1):
             for q in range(4):
                 nc.sync.dma_start(
                     out=dst[32 * q : 32 * q + 4, :, :].bitcast(I32),
-                    in_=src.bitcast(I32)[:, 4 * q : 4 * q + 4, :].rearrange("g r n -> r g n"),
+                    in_=src.bitcast(I32)[g0:g1, 4 * q : 4 * q + 4, :].rearrange("g r n -> r g n"),
                 )
 
         def load_a(z):
@@ -92,48 +99,70 @@ def tile_zoned_interbank_clearing_s14_kernel(
         def load_b(z):
             nc.sync.dma_start(out=b_t[z][:].bitcast(I32), in_=b_words.bitcast(I32)[z, :, :])
 
-        def load_owed(dst, src):
-            nc.sync.dma_start(out=dst[:], in_=src.rearrange("z (p t) -> p z t", t=4))
+        def load_owed():
+            nc.sync.dma_start(out=owed_rows[0:Z, :], in_=owed1)
+            nc.sync.dma_start(out=owed_rows[Z : 2 * Z, :], in_=owed2)
+
+        def turn_owed():
+            words = owed_rows[:].bitcast(F32)
+            for u in range(2):
+                nc.tensor.transpose(owed2_ps[:, u * P : (u + 1) * P], words[:, u:256:2], ident[:])
+            nc.scalar.copy(
+                out=owed_t[:].bitcast(F32),
+                in_=owed2_ps[:, 0 : 2 * P].rearrange("p (u i) -> p i u", u=2)[:, 0 : 2 * Z, :],
+            )
 
         def loads_needed_in(period):
-            n = period + 3
-            if 0 <= n < PAIRS:
-                load_pay(n)
             n = period + 2
-            if n == 0:
-                load_scales(a_sc, a_scales)
-            if 0 <= n < PAIRS and n % PER_ZONE == 0:
+            if n < PAIRS and n % PER_ZONE == 0:
                 load_a(n // PER_ZONE)
-            if 0 <= n < PAIRS:
-                load_cash(cash1_t, cash1, n)
-            if period == -1:
-                load_owed(owed1_t, owed1)
-                load_scales(b_sc, b_scales)
-            if 0 <= period < PAIRS and period % PER_ZONE == 0:
+            if period + 1 < PAIRS:
+                load_cash(cash1_t, cash1, period + 1)
+            if period < PAIRS and period % PER_ZONE == 0:
                 load_b(period // PER_ZONE)
-            if period == 0:
-                load_owed(owed2_t, owed2)
-            n = period - 1
-            if 0 <= n < PAIRS:
-                load_cash(cash2_t, cash2, n)
+            if period - 1 < PAIRS:
+                load_cash(cash2_t, cash2, period - 1)
+            if period == 2:
+                load_scales(a_sc_rest, a_scales, 2, 2 * Z)
+            if period + 4 < PAIRS:
+                load_pay(period + 4)
 
-        def transpose_pay(n, j, g):
-            words = pay_t[n][j][:].bitcast(F32)
-            for u in range(2):
-                c = (2 * g + u) * P
-                nc.tensor.transpose(
-                    payT_ps[j][:, c : c + P], words[:, 256 * g + u : 256 * (g + 1) : 2], ident[:]
-                )
+        def pay_words(n, j):
+            return pay_t[n][:, N * j : N * (j + 1)].bitcast(F32)
+
+        def sort_pay(n, j):
+            nc.scalar.copy(
+                out=sorted_t[j][:].rearrange("s (u c i) -> s c u i", u=2, i=4),
+                in_=pay_words(n, j).rearrange("s (c i u) -> s c u i", u=2, i=4),
+            )
+
+        def transpose_pay(n, j):
+            for g in range(2):
+                for u in range(2):
+                    if n == 0 or (n > 3 and j not in SORTED_TILES):
+                        words = pay_words(n, j)[:, 256 * g + u : 256 * (g + 1) : 2]
+                    else:
+                        words = sorted_t[j][:, 256 * u + P * g : 256 * u + P * (g + 1)]
+                    c = (2 * g + u) * P
+                    nc.tensor.transpose(payT_ps[j][:, c : c + P], words, ident[:])
 
         def copy_payT(n, j):
             nc.scalar.copy(
-                out=stage[n % 2][:, 512 * j : 512 * (j + 1)].rearrange("p (g s u) -> p g s u", g=2, u=2),
+                out=stage[n % 3][:, 512 * j : 512 * (j + 1)].rearrange("p (g s u) -> p g s u", g=2, u=2),
                 in_=payT_ps[j][:].rearrange("p (g u s) -> p g s u", g=2, u=2),
             )
 
         def quantize_pay(n):
             nc.vector.quantize_mx(
-                out=pay_codes[n % 2][:].bitcast(FP8X4), scales=pay_sc[n % 2][:], in_=stage[n % 2][:].bitcast(BF16)
+                out=pay_codes[n % 2][:].bitcast(FP8X4), scales=pay_sc[n % 2][:], in_=stage[n % 3][:].bitcast(BF16)
+            )
+
+        def quantize_pay_tile(n, j):
+            cols = slice(256 * j, 256 * (j + 1))
+            nc.vector.quantize_mx(
+                out=pay_codes[n % 2][:, cols].bitcast(FP8X4),
+                scales=pay_sc[n % 2][:, cols],
+                in_=stage[n % 3][:, 512 * j : 512 * (j + 1)].bitcast(BF16),
             )
 
         def matmul1(n, j, g):
@@ -144,7 +173,7 @@ def tile_zoned_interbank_clearing_s14_kernel(
                 lhsT=pay_codes[n % 2][:, cols].bitcast(FP8X4),
                 lhsT_scale=pay_sc[n % 2][:, cols],
                 rhs=a_t[z][:, g, :].bitcast(FP4X4),
-                rhs_scale=a_sc[:, 2 * z + g, :],
+                rhs_scale=a_sc[2 * z + g],
                 start=(g == 0),
                 stop=(g == 1),
             )
@@ -164,14 +193,17 @@ def tile_zoned_interbank_clearing_s14_kernel(
                 nc.tensor.transpose(haveT_ps[:, c : c + P], words[:, u * P : (u + 1) * P], ident[:])
 
         def paid_view(n):
-            return shared[n % 3][:, 0:512].bitcast(BF16)
+            return paid_t[n % 2][:, 0:512].bitcast(BF16)
+
+        def sums(n):
+            return stage[n % 3] if n + 3 < PAIRS else paid_t[(n + 1) % 2]
 
         def min_owed1(n):
             z = n // PER_ZONE
             nc.vector.tensor_tensor(
                 out=paid_view(n).rearrange("p (s u e) -> p s u e", u=2, e=2),
                 in0=haveT_ps[:].bitcast(BF16).rearrange("p (u s e) -> p s u e", u=2, e=2),
-                in1=owed1_t[:, z, :].rearrange("p (u e) -> p u e", e=2).unsqueeze(1).to_broadcast([P, PAIR, 2, 2]),
+                in1=owed_t[:, z, :].rearrange("p (u e) -> p u e", e=2).unsqueeze(1).to_broadcast([P, PAIR, 2, 2]),
                 op=MIN,
             )
 
@@ -195,86 +227,157 @@ def tile_zoned_interbank_clearing_s14_kernel(
             nc.scalar.copy(out=in2_sb[n % 2][:, R * j : R * (j + 1)], in_=in2_ps[j][:])
 
         def add_cash2_gpsimd(n):
-            nc.gpsimd.tensor_tensor(out=shared[(n + 1) % 3][:], in0=in2_sb[n % 2][:], in1=cash2_t[n][:], op=ADD)
+            nc.gpsimd.tensor_tensor(out=sums(n)[:], in0=in2_sb[n % 2][:], in1=cash2_t[n][:], op=ADD)
 
         def add_cash2_vector(n, j):
             cols = slice(R * j, R * (j + 1))
             nc.vector.tensor_tensor(out=in2_sb[n % 2][:, cols], in0=in2_ps[j][:], in1=cash2_t[n][:, cols], op=ADD)
 
         def spread_owed2(z):
-            for t in range(4):
-                c = 4 * z + t
-                nc.tensor.transpose(owed2_ps[:, t:R:4], owed2_f[:, c : c + 1].to_broadcast([P, P]), ident[:])
+            words = owed_t[:, Z + z, :].bitcast(F32)
+            for u in range(2):
+                nc.tensor.transpose(owed2_ps[:, u:256:2], words[:, u : u + 1].to_broadcast([P, P]), ident[:])
 
         def min_owed2_pair(n):
             nc.vector.tensor_tensor(
                 out=out_t[n % OUT_BUFS][:].rearrange("s (j r) -> s j r", j=2),
-                in0=shared[(n + 1) % 3][:].rearrange("s (j r) -> s j r", j=2),
-                in1=owed2_ps[:].unsqueeze(1).to_broadcast([P, 2, R]),
+                in0=sums(n)[:].rearrange("s (j r) -> s j r", j=2),
+                in1=owed2_row.unsqueeze(1).to_broadcast([P, 2, R]),
                 op=MIN,
             )
             nc.sync.dma_start(out=rows(out, n), in_=out_t[n % OUT_BUFS][:].rearrange("s (j r) -> s j r", j=2))
 
-        def min_owed2_tile(n, j):
+        def min_owed2_tile(n, j, total):
             cols = slice(R * j, R * (j + 1))
-            nc.vector.tensor_tensor(out=out_t[n % OUT_BUFS][:, cols], in0=in2_sb[n % 2][:, cols], in1=owed2_ps[:], op=MIN)
+            nc.vector.tensor_tensor(out=out_t[n % OUT_BUFS][:, cols], in0=total[:, cols], in1=owed2_row, op=MIN)
             nc.sync.dma_start(out=rows(out, n)[:, j, :], in_=out_t[n % OUT_BUFS][:, cols])
 
         def live(n, upto=PAIRS):
             return 0 <= n < upto
 
-        via_gpsimd = PAIRS - DIRECT
+        last = PAIRS - 1
 
-        nc.vector.memset(a_sc[:].rearrange("p g n -> p (g n)").bitcast(I32), 0)
-        nc.vector.memset(b_sc[:].rearrange("p g n -> p (g n)").bitcast(I32), 0)
+        def zero(plane):
+            nc.vector.memset(plane[:].rearrange("p g n -> p (g n)").bitcast(I32), 0)
+
+        zero(a_sc_first)
         make_identity(nc, ident[:])
-        for period in range(-3, -3 + LEAD):
+        nc.vector.memset(owed_rows[:].bitcast(F32), 0.0)
+        zero(b_sc)
+        zero(a_sc_rest)
+        load_pay(0)
+        load_scales(a_sc_first, a_scales, 0, 2)
+        load_a(0)
+        load_pay(1)
+        load_cash(cash1_t, cash1, 0)
+        load_pay(2)
+        load_cash(cash1_t, cash1, 1)
+        load_owed()
+        load_pay(3)
+        load_scales(b_sc, b_scales, 0, Z)
+        load_b(0)
+        load_pay(4)
+        for period in range(1, 1 + LEAD):
             loads_needed_in(period)
 
-        for w in range(-3, PAIRS):
+        def matmul1_tile(n, j):
+            matmul1(n, j, 0)
+            matmul1(n, j, 1)
+
+        def transpose_and_copy(n, j):
+            transpose_pay(n, j)
+            copy_payT(n, j)
+
+        for j in range(2):
+            transpose_and_copy(0, j)
+            quantize_pay_tile(0, j)
+        sort_pay(1, 0)
+        sort_pay(1, 1)
+        matmul1_tile(0, 0)
+        add_cash1(0, 0)
+        transpose_and_copy(1, 0)
+        matmul1_tile(0, 1)
+        quantize_pay_tile(1, 0)
+        add_cash1(0, 1)
+        sort_pay(2, 0)
+        transpose_and_copy(1, 1)
+        turn_owed()
+        sort_pay(2, 1)
+        matmul1_tile(1, 0)
+        quantize_pay_tile(1, 1)
+        transpose_have(0)
+        transpose_have(1)
+        add_cash1(1, 0)
+        min_owed1(0)
+        transpose_and_copy(2, 0)
+        sort_pay(3, 0)
+        matmul1_tile(1, 1)
+        quantize_pay_tile(2, 0)
+        quantize_paid(0)
+        add_cash1(1, 1)
+        transpose_and_copy(2, 1)
+        sort_pay(3, 1)
+        matmul1_tile(2, 0)
+        quantize_pay_tile(2, 1)
+        transpose_and_copy(3, 0)
+        transpose_have(0)
+        transpose_have(1)
+        min_owed1(1)
+        transpose_and_copy(3, 1)
+        add_cash1(2, 0)
+        matmul2(0, 0)
+        matmul2(0, 1)
+        matmul1_tile(2, 1)
+        for j in range(2):
+            copy_in2(0, j)
+        for j in SORTED_TILES:
+            sort_pay(4, j)
+        transpose_pay(4, 0)
+
+        for w in range(1, PAIRS):
             loads_needed_in(w + LEAD)
             if live(w + 2):
                 quantize_pay(w + 2)
-            if live(w):
-                quantize_paid(w)
-            if live(w - 1, via_gpsimd):
+            quantize_paid(w)
+            if w - 1 >= FIRST_G:
                 add_cash2_gpsimd(w - 1)
             if live(w + 3):
-                transpose_pay(w + 3, 0, 0)
-            if live(w + 1):
-                transpose_have(1)
-                min_owed1(w + 1)
-            if w == 0:
-                nc.scalar.copy(out=owed2_f[:], in_=owed2_t[:].rearrange("p z t -> p (z t)"))
-            if live(w - 2) and (w - 2) % PER_ZONE == 0:
-                spread_owed2((w - 2) // PER_ZONE)
-            if live(w + 3):
-                transpose_pay(w + 3, 0, 1)
                 copy_payT(w + 3, 0)
-            if live(w + 2):
-                matmul1(w + 2, 0, 0)
-                matmul1(w + 2, 0, 1)
-                matmul1(w + 2, 1, 0)
-            if live(w + 3):
-                transpose_pay(w + 3, 1, 0)
-                transpose_pay(w + 3, 1, 1)
-                copy_payT(w + 3, 1)
-            if live(w + 2):
-                matmul1(w + 2, 1, 1)
-            if live(w):
-                matmul2(w, 0)
-                matmul2(w, 1)
-            if live(w, via_gpsimd):
+            matmul2(w, 0)
+            matmul2(w, 1)
+            if live(w + 4) and 0 in SORTED_TILES:
+                sort_pay(w + 4, 0)
+            if 1 < w < last:
+                add_cash1(w + 1, 0)
+            if w < last:
+                add_cash1(w + 1, 1)
+            if w < last:
                 copy_in2(w, 0)
+            if live(w + 3):
+                transpose_pay(w + 3, 1)
+                copy_payT(w + 3, 1)
+            if w < last:
                 copy_in2(w, 1)
-            if live(w - 2, via_gpsimd):
-                min_owed2_pair(w - 2)
-            if live(w + 2):
-                add_cash1(w + 2, 0)
-                add_cash1(w + 2, 1)
+            if live(w + 1):
                 transpose_have(0)
-            if live(w) and w >= via_gpsimd:
-                add_cash2_vector(w, 0)
-                add_cash2_vector(w, 1)
-                min_owed2_tile(w, 0)
-                min_owed2_tile(w, 1)
+                transpose_have(1)
+            if w - 2 >= FIRST_G:
+                min_owed2_pair(w - 2)
+            if live(w + 1):
+                min_owed1(w + 1)
+            if live(w + 2):
+                matmul1_tile(w + 2, 0)
+                matmul1_tile(w + 2, 1)
+            if live(w + 4) and 1 in SORTED_TILES:
+                sort_pay(w + 4, 1)
+            if live(w + 4):
+                transpose_pay(w + 4, 0)
+            if w - 1 >= FIRST_G and (w - 1) % PER_ZONE == 0:
+                spread_owed2((w - 1) // PER_ZONE)
+
+        for j in range(2):
+            add_cash2_vector(last, j)
+        for j in range(2):
+            min_owed2_tile(last, j, in2_sb[last % 2])
+        for j in range(2):
+            min_owed2_tile(last - 1, j, sums(last - 1))

@@ -19,11 +19,14 @@ MIN = mybir.AluOpType.min
 P = 128
 PAIR = 2 * P
 PAIRS = Z * S // PAIR
-PER_ZONE = S // PAIR
+PAIRS_PER_ZONE = S // PAIR
+LAST = PAIRS - 1
+K_PASS = 512
+DUOS = K_PASS // 2
+PASSES1 = N // K_PASS
+BANK = 512
 LEAD = 5
-OUT_BUFS = 6
-SORTED_TILES = (1,)
-FIRST_G = 0
+HEAD_PAIRS = 4
 
 
 def tile_zoned_interbank_clearing_s14_kernel(
@@ -31,187 +34,188 @@ def tile_zoned_interbank_clearing_s14_kernel(
 ):
     nc = tc.nc
 
-    def rows(t, n):
-        z, q = divmod(n, PER_ZONE)
-        return t[z, q * PAIR : (q + 1) * PAIR, :].rearrange("(p j) k -> p j k", j=2)
+    def rows(tensor, n):
+        z, q = divmod(n, PAIRS_PER_ZONE)
+        return tensor[z, q * PAIR : (q + 1) * PAIR, :].rearrange("(p j) k -> p j k", j=2)
 
     with ExitStack() as ctx:
         sb = ctx.enter_context(tc.tile_pool(name="sb", bufs=1))
         ps = ctx.enter_context(tc.psum_pool(name="ps", bufs=1))
         ctx.enter_context(tc.manual_schedule())
 
-        def ring(name, count, shape, dtype):
+        def tiles(name, count, shape, dtype):
             return [sb.tile(shape, dtype, name="%s%d" % (name, i), align_bytes=64) for i in range(count)]
 
         ident = sb.tile([P, P], F32)
-        pay_t = ring("pay", PAIRS, [P, 2 * N], BF16)
-        sorted_t = ring("sorted", 2, [P, 512], F32)
-        cash1_t = ring("cash1_", PAIRS, [P, 2 * M], BF16)
-        cash2_t = ring("cash2_", PAIRS, [P, 2 * R], BF16)
-        a_t = ring("a", Z, [P, 2, 2 * M], U8)
-        b_t = ring("b", Z, [P, 2 * R], U8)
-        a_sc_first = sb.tile([P, 2, M], U8, align_bytes=64)
-        a_sc_rest = sb.tile([P, 2 * (Z - 1), M], U8, align_bytes=64)
+
+        pay_t = tiles("pay", PAIRS, [P, 2 * N], BF16)
+        sorted_t = tiles("sorted", 2, [P, PASSES1 * DUOS], F32)
+        cash1_two = tiles("cash1_", PAIRS // 2, [P, 4 * M], BF16)
+        cash1_t = [cash1_two[n // 2][:, 2 * M * (n % 2) : 2 * M * (n % 2 + 1)] for n in range(PAIRS)]
+        cash2_t = tiles("cash2_", PAIRS, [P, 2 * R], BF16)
+        a_t = tiles("a", Z, [P, PASSES1, 2 * M], U8)
+        b_t = tiles("b", Z, [P, 2 * R], U8)
+        a_sc_first = sb.tile([P, PASSES1, M], U8, align_bytes=64)
+        a_sc_rest = sb.tile([P, PASSES1 * (Z - 1), M], U8, align_bytes=64)
+        a_sc = [a_sc_first[:, g, :] for g in range(PASSES1)] + [a_sc_rest[:, g, :] for g in range(PASSES1 * (Z - 1))]
         b_sc = sb.tile([P, Z, R], U8, align_bytes=64)
-        a_sc = [a_sc_first[:, g, :] for g in range(2)] + [a_sc_rest[:, g, :] for g in range(2 * (Z - 1))]
         owed_rows = sb.tile([P, M], BF16)
         owed_t = sb.tile([P, 2 * Z, 4], BF16)
-        stage = ring("stage", 3, [P, 1024], F32)
-        pay_codes = ring("pay_codes", 2, [P, 512], U32)
-        pay_sc = ring("pay_sc", 2, [P, 512], U8)
-        paid_codes = ring("paid_codes", 2, [P, 256], U32)
-        paid_sc = ring("paid_sc", 2, [P, 256], U8)
-        have1 = ring("have1_", 2, [P, M], BF16)
-        paid_t = ring("paid", 2, [P, 1024], F32)
-        in2_sb = ring("in2_sb", 2, [P, 1024], F32)
-        out_t = ring("out_t", OUT_BUFS, [P, 1024], F32)
 
-        payT_ps = [ps.tile([P, 512], F32, name="payT%d" % j) for j in range(2)]
-        in1_ps = [ps.tile([P, 512], F32, name="in1_%d" % j) for j in range(2)]
-        in2_ps = [ps.tile([P, 512], F32, name="in2_%d" % j) for j in range(2)]
-        haveT_ps = ps.tile([P, 512], F32)
-        owed2_ps = ps.tile([P, 512], F32)
-        owed2_row = owed2_ps[:, 0:256].bitcast(BF16)
+        stage = tiles("stage", 3, [P, 2 * PASSES1 * DUOS], F32)
+        pay_codes = tiles("pay_codes", 2, [P, 2 * PASSES1 * P], U32)
+        pay_sc = tiles("pay_sc", 2, [P, 2 * PASSES1 * P], U8)
+        paid_codes = tiles("paid_codes", 2, [P, PAIR], U32)
+        paid_sc = tiles("paid_sc", 2, [P, PAIR], U8)
+        have1 = tiles("have1_", 4, [P, M], BF16)
+        paid_t = tiles("paid", 2, [P, 2 * R], F32)
+        in2_sb = tiles("in2_sb", 2, [P, 2 * R], F32)
 
-        def load_pay(n):
-            if n < 2:
-                for j in range(2):
-                    nc.sync.dma_start(out=pay_t[n][:, N * j : N * (j + 1)], in_=rows(pay, n)[:, j, :])
-            else:
-                nc.sync.dma_start(out=pay_t[n][:].rearrange("p (j k) -> p j k", j=2), in_=rows(pay, n))
+        pay_ps = [ps.tile([P, BANK], F32, name="pay_ps%d" % j) for j in range(2)]
+        in1_ps = [ps.tile([P, BANK], F32, name="in1_ps%d" % j) for j in range(2)]
+        in2_ps = [ps.tile([P, BANK], F32, name="in2_ps%d" % j) for j in range(2)]
+        have_ps = ps.tile([P, BANK], F32)
+        owed2_ps = ps.tile([P, BANK], F32)
+        owed2_row = owed2_ps[:, 0:DUOS].bitcast(BF16)
 
-        def load_cash(dst, src, n):
-            nc.sync.dma_start(out=dst[n][:].rearrange("p (j k) -> p j k", j=2), in_=rows(src, n))
+        def live(n):
+            return 0 <= n < PAIRS
 
-        def load_scales(dst, src, g0, g1):
+        def load_pay_columns(n, j, k0, k1):
+            nc.sync.dma_start(out=pay_t[n][:, N * j + k0 : N * j + k1], in_=rows(pay, n)[:, j, k0:k1])
+
+        def load_pair(dst, tensor, n):
+            nc.sync.dma_start(out=dst[n][:].rearrange("p (j k) -> p j k", j=2), in_=rows(tensor, n))
+
+        def load_cash1_two_pairs(n):
+            z, q = divmod(n, PAIRS_PER_ZONE)
+            nc.sync.dma_start(
+                out=cash1_two[n // 2][:].rearrange("p (h k) -> p h k", h=2),
+                in_=cash1[z, q * PAIR : (q + 2) * PAIR, :].rearrange("(h p j) k -> p h (j k)", h=2, j=2),
+            )
+
+        def load_scales(plane, scales, g0, g1):
             for q in range(4):
                 nc.sync.dma_start(
-                    out=dst[32 * q : 32 * q + 4, :, :].bitcast(I32),
-                    in_=src.bitcast(I32)[g0:g1, 4 * q : 4 * q + 4, :].rearrange("g r n -> r g n"),
+                    out=plane[32 * q : 32 * q + 4, :, :].bitcast(I32),
+                    in_=scales.bitcast(I32)[g0:g1, 4 * q : 4 * q + 4, :].rearrange("g r n -> r g n"),
                 )
 
         def load_a(z):
             nc.sync.dma_start(
                 out=a_t[z][:].bitcast(I32),
-                in_=a_words.bitcast(I32)[2 * z : 2 * z + 2, :, :].rearrange("g p n -> p g n"),
+                in_=a_words.bitcast(I32)[PASSES1 * z : PASSES1 * (z + 1), :, :].rearrange("g p n -> p g n"),
             )
 
         def load_b(z):
             nc.sync.dma_start(out=b_t[z][:].bitcast(I32), in_=b_words.bitcast(I32)[z, :, :])
 
-        def load_owed():
-            nc.sync.dma_start(out=owed_rows[0:Z, :], in_=owed1)
-            nc.sync.dma_start(out=owed_rows[Z : 2 * Z, :], in_=owed2)
+        def loads_for_step(w):
+            if live(w + 2) and (w + 2) % PAIRS_PER_ZONE == 0:
+                load_a((w + 2) // PAIRS_PER_ZONE)
+            if live(w + 2) and w % 2 == 0:
+                load_cash1_two_pairs(w + 2)
+            if live(w) and w % PAIRS_PER_ZONE == 0:
+                load_b(w // PAIRS_PER_ZONE)
+            if live(w - 1):
+                load_pair(cash2_t, cash2, w - 1)
+            if w + 2 == PAIRS_PER_ZONE:
+                load_scales(a_sc_rest, a_scales, PASSES1, PASSES1 * Z)
+            if live(w + 4):
+                load_pair(pay_t, pay, w + 4)
 
-        def turn_owed():
-            words = owed_rows[:].bitcast(F32)
-            for u in range(2):
-                nc.tensor.transpose(owed2_ps[:, u * P : (u + 1) * P], words[:, u:256:2], ident[:])
-            nc.scalar.copy(
-                out=owed_t[:].bitcast(F32),
-                in_=owed2_ps[:, 0 : 2 * P].rearrange("p (u i) -> p i u", u=2)[:, 0 : 2 * Z, :],
-            )
-
-        def loads_needed_in(period):
-            n = period + 2
-            if n < PAIRS and n % PER_ZONE == 0:
-                load_a(n // PER_ZONE)
-            if period + 1 < PAIRS:
-                load_cash(cash1_t, cash1, period + 1)
-            if period < PAIRS and period % PER_ZONE == 0:
-                load_b(period // PER_ZONE)
-            if period - 1 < PAIRS:
-                load_cash(cash2_t, cash2, period - 1)
-            if period == 2:
-                load_scales(a_sc_rest, a_scales, 2, 2 * Z)
-            if period + 4 < PAIRS:
-                load_pay(period + 4)
-
-        def pay_words(n, j):
+        def pay_duos(n, j):
             return pay_t[n][:, N * j : N * (j + 1)].bitcast(F32)
+
+        def every_second_duo(n, j, g, u):
+            return pay_duos(n, j)[:, DUOS * g + u : DUOS * (g + 1) : 2]
+
+        def is_sorted(n, j):
+            return n > 0 and (n < HEAD_PAIRS or j == 1)
 
         def sort_pay(n, j):
             nc.scalar.copy(
                 out=sorted_t[j][:].rearrange("s (u c i) -> s c u i", u=2, i=4),
-                in_=pay_words(n, j).rearrange("s (c i u) -> s c u i", u=2, i=4),
+                in_=pay_duos(n, j).rearrange("s (c i u) -> s c u i", u=2, i=4),
             )
 
-        def transpose_pay(n, j):
-            for g in range(2):
+        def transpose_pay(n, j, bank):
+            for g in range(PASSES1):
                 for u in range(2):
-                    if n == 0 or (n > 3 and j not in SORTED_TILES):
-                        words = pay_words(n, j)[:, 256 * g + u : 256 * (g + 1) : 2]
+                    if is_sorted(n, j):
+                        duos = sorted_t[j][:, DUOS * u + P * g : DUOS * u + P * (g + 1)]
                     else:
-                        words = sorted_t[j][:, 256 * u + P * g : 256 * u + P * (g + 1)]
+                        duos = every_second_duo(n, j, g, u)
                     c = (2 * g + u) * P
-                    nc.tensor.transpose(payT_ps[j][:, c : c + P], words, ident[:])
+                    nc.tensor.transpose(pay_ps[bank][:, c : c + P], duos, ident[:])
 
-        def copy_payT(n, j):
+        def copy_turned_pay(n, j, bank):
             nc.scalar.copy(
-                out=stage[n % 3][:, 512 * j : 512 * (j + 1)].rearrange("p (g s u) -> p g s u", g=2, u=2),
-                in_=payT_ps[j][:].rearrange("p (g u s) -> p g s u", g=2, u=2),
+                out=stage[n % 3][:, BANK * j : BANK * (j + 1)].rearrange("p (g s u) -> p g s u", g=PASSES1, u=2),
+                in_=pay_ps[bank][:].rearrange("p (g u s) -> p g s u", g=PASSES1, u=2),
             )
 
-        def quantize_pay(n):
-            nc.vector.quantize_mx(
-                out=pay_codes[n % 2][:].bitcast(FP8X4), scales=pay_sc[n % 2][:], in_=stage[n % 3][:].bitcast(BF16)
-            )
+        def turn_pay(n, j):
+            transpose_pay(n, j, bank=j)
+            copy_turned_pay(n, j, bank=j)
 
-        def quantize_pay_tile(n, j):
-            cols = slice(256 * j, 256 * (j + 1))
+        def quantize_pay(n, first, count):
+            cols = slice(first * P, (first + count) * P)
             nc.vector.quantize_mx(
                 out=pay_codes[n % 2][:, cols].bitcast(FP8X4),
                 scales=pay_sc[n % 2][:, cols],
-                in_=stage[n % 3][:, 512 * j : 512 * (j + 1)].bitcast(BF16),
+                in_=stage[n % 3][:, first * DUOS : (first + count) * DUOS].bitcast(BF16),
             )
 
-        def matmul1(n, j, g):
-            z = n // PER_ZONE
-            cols = slice((2 * j + g) * P, (2 * j + g + 1) * P)
-            nc.tensor.matmul_mx(
-                out=in1_ps[j][:],
-                lhsT=pay_codes[n % 2][:, cols].bitcast(FP8X4),
-                lhsT_scale=pay_sc[n % 2][:, cols],
-                rhs=a_t[z][:, g, :].bitcast(FP4X4),
-                rhs_scale=a_sc[2 * z + g],
-                start=(g == 0),
-                stop=(g == 1),
-            )
+        def quantize_pay_tile(n, j):
+            quantize_pay(n, PASSES1 * j, PASSES1)
+
+        def matmul1(n, j):
+            z = n // PAIRS_PER_ZONE
+            for g in range(PASSES1):
+                cols = slice((PASSES1 * j + g) * P, (PASSES1 * j + g + 1) * P)
+                nc.tensor.matmul_mx(
+                    out=in1_ps[j][:],
+                    lhsT=pay_codes[n % 2][:, cols].bitcast(FP8X4),
+                    lhsT_scale=pay_sc[n % 2][:, cols],
+                    rhs=a_t[z][:, g, :].bitcast(FP4X4),
+                    rhs_scale=a_sc[PASSES1 * z + g],
+                    start=(g == 0),
+                    stop=(g == PASSES1 - 1),
+                )
 
         def add_cash1(n, j):
             nc.vector.tensor_tensor(
-                out=have1[j][:].rearrange("s (u p e) -> s u p e", u=2, e=2),
+                out=have1[2 * (n % 2) + j][:].rearrange("s (u p e) -> s u p e", u=2, e=2),
                 in0=in1_ps[j][:].rearrange("s (p u e) -> s u p e", u=2, e=2),
                 in1=cash1_t[n][:, M * j : M * (j + 1)].rearrange("s (p u e) -> s u p e", u=2, e=2),
                 op=ADD,
             )
 
-        def transpose_have(j):
-            words = have1[j][:].bitcast(F32)
-            for u in range(2):
-                c = (2 * u + j) * P
-                nc.tensor.transpose(haveT_ps[:, c : c + P], words[:, u * P : (u + 1) * P], ident[:])
+        def transpose_have(n):
+            for j in range(2):
+                duos = have1[2 * (n % 2) + j][:].bitcast(F32)
+                for u in range(2):
+                    c = (2 * u + j) * P
+                    nc.tensor.transpose(have_ps[:, c : c + P], duos[:, u * P : (u + 1) * P], ident[:])
 
-        def paid_view(n):
-            return paid_t[n % 2][:, 0:512].bitcast(BF16)
-
-        def sums(n):
-            return stage[n % 3] if n + 3 < PAIRS else paid_t[(n + 1) % 2]
+        def paid1(n):
+            return paid_t[n % 2][:, 0:R].bitcast(BF16)
 
         def min_owed1(n):
-            z = n // PER_ZONE
+            z = n // PAIRS_PER_ZONE
             nc.vector.tensor_tensor(
-                out=paid_view(n).rearrange("p (s u e) -> p s u e", u=2, e=2),
-                in0=haveT_ps[:].bitcast(BF16).rearrange("p (u s e) -> p s u e", u=2, e=2),
+                out=paid1(n).rearrange("p (s u e) -> p s u e", u=2, e=2),
+                in0=have_ps[:].bitcast(BF16).rearrange("p (u s e) -> p s u e", u=2, e=2),
                 in1=owed_t[:, z, :].rearrange("p (u e) -> p u e", e=2).unsqueeze(1).to_broadcast([P, PAIR, 2, 2]),
                 op=MIN,
             )
 
         def quantize_paid(n):
-            nc.vector.quantize_mx(out=paid_codes[n % 2][:].bitcast(FP8X4), scales=paid_sc[n % 2][:], in_=paid_view(n))
+            nc.vector.quantize_mx(out=paid_codes[n % 2][:].bitcast(FP8X4), scales=paid_sc[n % 2][:], in_=paid1(n))
 
         def matmul2(n, j):
-            z = n // PER_ZONE
+            z = n // PAIRS_PER_ZONE
             cols = slice(j * P, (j + 1) * P)
             nc.tensor.matmul_mx(
                 out=in2_ps[j][:],
@@ -226,6 +230,9 @@ def tile_zoned_interbank_clearing_s14_kernel(
         def copy_in2(n, j):
             nc.scalar.copy(out=in2_sb[n % 2][:, R * j : R * (j + 1)], in_=in2_ps[j][:])
 
+        def sums(n):
+            return stage[n % 3] if live(n + 3) else paid_t[(n + 1) % 2]
+
         def add_cash2_gpsimd(n):
             nc.gpsimd.tensor_tensor(out=sums(n)[:], in0=in2_sb[n % 2][:], in1=cash2_t[n][:], op=ADD)
 
@@ -233,29 +240,35 @@ def tile_zoned_interbank_clearing_s14_kernel(
             cols = slice(R * j, R * (j + 1))
             nc.vector.tensor_tensor(out=in2_sb[n % 2][:, cols], in0=in2_ps[j][:], in1=cash2_t[n][:, cols], op=ADD)
 
-        def spread_owed2(z):
-            words = owed_t[:, Z + z, :].bitcast(F32)
+        def turn_owed():
+            duos = owed_rows[:].bitcast(F32)
             for u in range(2):
-                nc.tensor.transpose(owed2_ps[:, u:256:2], words[:, u : u + 1].to_broadcast([P, P]), ident[:])
+                nc.tensor.transpose(owed2_ps[:, u * P : (u + 1) * P], duos[:, u:DUOS:2], ident[:])
+            nc.scalar.copy(
+                out=owed_t[:].bitcast(F32),
+                in_=owed2_ps[:, 0 : 2 * P].rearrange("p (u i) -> p i u", u=2)[:, 0 : 2 * Z, :],
+            )
 
-        def min_owed2_pair(n):
+        def spread_owed2(z):
+            duos = owed_t[:, Z + z, :].bitcast(F32)
+            for u in range(2):
+                nc.tensor.transpose(owed2_ps[:, u:DUOS:2], duos[:, u : u + 1].to_broadcast([P, P]), ident[:])
+
+        def finish_pair(n):
+            result = pay_t[n][:].bitcast(F32).rearrange("s (j r) -> s j r", j=2)
             nc.vector.tensor_tensor(
-                out=out_t[n % OUT_BUFS][:].rearrange("s (j r) -> s j r", j=2),
+                out=result,
                 in0=sums(n)[:].rearrange("s (j r) -> s j r", j=2),
                 in1=owed2_row.unsqueeze(1).to_broadcast([P, 2, R]),
                 op=MIN,
             )
-            nc.sync.dma_start(out=rows(out, n), in_=out_t[n % OUT_BUFS][:].rearrange("s (j r) -> s j r", j=2))
+            nc.sync.dma_start(out=rows(out, n), in_=result)
 
-        def min_owed2_tile(n, j, total):
-            cols = slice(R * j, R * (j + 1))
-            nc.vector.tensor_tensor(out=out_t[n % OUT_BUFS][:, cols], in0=total[:, cols], in1=owed2_row, op=MIN)
-            nc.sync.dma_start(out=rows(out, n)[:, j, :], in_=out_t[n % OUT_BUFS][:, cols])
-
-        def live(n, upto=PAIRS):
-            return 0 <= n < upto
-
-        last = PAIRS - 1
+        def finish_columns(n, j, total, r0, r1):
+            cols = slice(R * j + r0, R * j + r1)
+            result = pay_t[n][:].bitcast(F32)[:, cols]
+            nc.vector.tensor_tensor(out=result, in0=total[:, cols], in1=owed2_row[:, r0:r1], op=MIN)
+            nc.sync.dma_start(out=rows(out, n)[:, j, r0:r1], in_=result)
 
         def zero(plane):
             nc.vector.memset(plane[:].rearrange("p g n -> p (g n)").bitcast(I32), 0)
@@ -265,119 +278,124 @@ def tile_zoned_interbank_clearing_s14_kernel(
         nc.vector.memset(owed_rows[:].bitcast(F32), 0.0)
         zero(b_sc)
         zero(a_sc_rest)
-        load_pay(0)
-        load_scales(a_sc_first, a_scales, 0, 2)
+
+        for g in range(PASSES1):
+            load_pay_columns(0, 0, K_PASS * g, K_PASS * (g + 1))
+        load_pay_columns(0, 1, 0, N)
+        load_scales(a_sc_first, a_scales, 0, PASSES1)
         load_a(0)
-        load_pay(1)
-        load_cash(cash1_t, cash1, 0)
-        load_pay(2)
-        load_cash(cash1_t, cash1, 1)
-        load_owed()
-        load_pay(3)
+        for j in range(2):
+            load_pay_columns(1, j, 0, N)
+        load_pair(cash1_t, cash1, 0)
+        load_pair(pay_t, pay, 2)
+        load_pair(cash1_t, cash1, 1)
+        nc.sync.dma_start(out=owed_rows[0:Z, :], in_=owed1)
+        nc.sync.dma_start(out=owed_rows[Z : 2 * Z, :], in_=owed2)
+        load_pair(pay_t, pay, 3)
         load_scales(b_sc, b_scales, 0, Z)
         load_b(0)
-        load_pay(4)
-        for period in range(1, 1 + LEAD):
-            loads_needed_in(period)
+        load_pair(pay_t, pay, 4)
+        load_cash1_two_pairs(2)
+        for w in range(1, 1 + LEAD):
+            loads_for_step(w)
 
-        def matmul1_tile(n, j):
-            matmul1(n, j, 0)
-            matmul1(n, j, 1)
-
-        def transpose_and_copy(n, j):
-            transpose_pay(n, j)
-            copy_payT(n, j)
-
-        for j in range(2):
-            transpose_and_copy(0, j)
-            quantize_pay_tile(0, j)
+        for g in range(PASSES1):
+            for u in range(2):
+                nc.tensor.transpose(pay_ps[g][:, u * P : (u + 1) * P], every_second_duo(0, 0, g, u), ident[:])
+            nc.scalar.copy(
+                out=stage[0][:, DUOS * g : DUOS * (g + 1)].rearrange("p (s u) -> p s u", u=2),
+                in_=pay_ps[g][:, 0 : 2 * P].rearrange("p (u s) -> p s u", u=2),
+            )
+            quantize_pay(0, g, 1)
+        transpose_pay(0, 1, bank=0)
+        copy_turned_pay(0, 1, bank=0)
+        quantize_pay_tile(0, 1)
         sort_pay(1, 0)
         sort_pay(1, 1)
-        matmul1_tile(0, 0)
+
+        matmul1(0, 0)
         add_cash1(0, 0)
-        transpose_and_copy(1, 0)
-        matmul1_tile(0, 1)
+        turn_pay(1, 0)
+
+        matmul1(0, 1)
         quantize_pay_tile(1, 0)
         add_cash1(0, 1)
         sort_pay(2, 0)
-        transpose_and_copy(1, 1)
+        turn_pay(1, 1)
         turn_owed()
         sort_pay(2, 1)
-        matmul1_tile(1, 0)
+
+        matmul1(1, 0)
         quantize_pay_tile(1, 1)
         transpose_have(0)
-        transpose_have(1)
         add_cash1(1, 0)
         min_owed1(0)
-        transpose_and_copy(2, 0)
+        turn_pay(2, 0)
         sort_pay(3, 0)
-        matmul1_tile(1, 1)
+
+        matmul1(1, 1)
         quantize_pay_tile(2, 0)
         quantize_paid(0)
         add_cash1(1, 1)
-        transpose_and_copy(2, 1)
+        turn_pay(2, 1)
         sort_pay(3, 1)
-        matmul1_tile(2, 0)
+
+        matmul1(2, 0)
         quantize_pay_tile(2, 1)
-        transpose_and_copy(3, 0)
-        transpose_have(0)
+        turn_pay(3, 0)
         transpose_have(1)
         min_owed1(1)
-        transpose_and_copy(3, 1)
+        turn_pay(3, 1)
         add_cash1(2, 0)
-        matmul2(0, 0)
-        matmul2(0, 1)
-        matmul1_tile(2, 1)
+
+        for j in range(2):
+            matmul2(0, j)
+        matmul1(2, 1)
         for j in range(2):
             copy_in2(0, j)
-        for j in SORTED_TILES:
-            sort_pay(4, j)
-        transpose_pay(4, 0)
+        sort_pay(4, 1)
+        transpose_pay(4, 0, bank=0)
 
         for w in range(1, PAIRS):
-            loads_needed_in(w + LEAD)
+            loads_for_step(w + LEAD)
             if live(w + 2):
-                quantize_pay(w + 2)
+                quantize_pay(w + 2, 0, 2 * PASSES1)
             quantize_paid(w)
-            if w - 1 >= FIRST_G:
-                add_cash2_gpsimd(w - 1)
+            add_cash2_gpsimd(w - 1)
             if live(w + 3):
-                copy_payT(w + 3, 0)
+                copy_turned_pay(w + 3, 0, bank=0)
+            if live(w + 2):
+                matmul1(w + 2, 0)
             matmul2(w, 0)
-            matmul2(w, 1)
-            if live(w + 4) and 0 in SORTED_TILES:
-                sort_pay(w + 4, 0)
-            if 1 < w < last:
-                add_cash1(w + 1, 0)
-            if w < last:
+            if live(w + 1):
                 add_cash1(w + 1, 1)
-            if w < last:
+            if w < LAST:
                 copy_in2(w, 0)
             if live(w + 3):
-                transpose_pay(w + 3, 1)
-                copy_payT(w + 3, 1)
-            if w < last:
-                copy_in2(w, 1)
+                turn_pay(w + 3, 1)
             if live(w + 1):
-                transpose_have(0)
-                transpose_have(1)
-            if w - 2 >= FIRST_G:
-                min_owed2_pair(w - 2)
+                transpose_have(w + 1)
+            if live(w - 2):
+                finish_pair(w - 2)
+            if live(w + 2):
+                add_cash1(w + 2, 0)
             if live(w + 1):
                 min_owed1(w + 1)
+            matmul2(w, 1)
             if live(w + 2):
-                matmul1_tile(w + 2, 0)
-                matmul1_tile(w + 2, 1)
-            if live(w + 4) and 1 in SORTED_TILES:
-                sort_pay(w + 4, 1)
+                matmul1(w + 2, 1)
+            if w < LAST:
+                copy_in2(w, 1)
             if live(w + 4):
-                transpose_pay(w + 4, 0)
-            if w - 1 >= FIRST_G and (w - 1) % PER_ZONE == 0:
-                spread_owed2((w - 1) // PER_ZONE)
+                sort_pay(w + 4, 1)
+                transpose_pay(w + 4, 0, bank=0)
+            if (w - 1) % PAIRS_PER_ZONE == 0:
+                spread_owed2((w - 1) // PAIRS_PER_ZONE)
 
         for j in range(2):
-            add_cash2_vector(last, j)
+            add_cash2_vector(LAST, j)
         for j in range(2):
-            min_owed2_tile(last, j, in2_sb[last % 2])
-        for j in range(2):
-            min_owed2_tile(last - 1, j, sums(last - 1))
+            finish_columns(LAST, j, in2_sb[LAST % 2], 0, R)
+        finish_columns(LAST - 1, 0, sums(LAST - 1), 0, R)
+        for half in range(2):
+            finish_columns(LAST - 1, 1, sums(LAST - 1), half * R // 2, (half + 1) * R // 2)

from contextlib import ExitStack

import concourse.mybir as mybir
from concourse.masks import make_identity

Z, S, N, M, R = 4, 1024, 1024, 512, 512
FLOPS = 2 * Z * S * (N * M + M * R)

F32 = mybir.dt.float32
BF16 = mybir.dt.bfloat16
I32 = mybir.dt.int32
U32 = mybir.dt.uint32
U8 = mybir.dt.uint8
FP8X4 = mybir.dt.float8_e4m3fn_x4
FP4X4 = mybir.dt.float4_e2m1fn_x4
ADD = mybir.AluOpType.add
MIN = mybir.AluOpType.min

P = 128
PAIR = 2 * P
PAIRS = Z * S // PAIR
PAIRS_PER_ZONE = S // PAIR
LAST = PAIRS - 1
K_PASS = 512
DUOS = K_PASS // 2
PASSES1 = N // K_PASS
BANK = 512
LEAD = 5
HEAD_PAIRS = 4


def tile_zoned_interbank_clearing_s14_kernel(
    tc, pay, a_words, a_scales, b_words, b_scales, cash1, owed1, cash2, owed2, out
):
    nc = tc.nc

    def rows(tensor, n):
        z, q = divmod(n, PAIRS_PER_ZONE)
        return tensor[z, q * PAIR : (q + 1) * PAIR, :].rearrange("(p j) k -> p j k", j=2)

    with ExitStack() as ctx:
        sb = ctx.enter_context(tc.tile_pool(name="sb", bufs=1))
        ps = ctx.enter_context(tc.psum_pool(name="ps", bufs=1))
        ctx.enter_context(tc.manual_schedule())

        def tiles(name, count, shape, dtype):
            return [sb.tile(shape, dtype, name="%s%d" % (name, i), align_bytes=64) for i in range(count)]

        ident = sb.tile([P, P], F32)

        pay_t = tiles("pay", PAIRS, [P, 2 * N], BF16)
        sorted_t = tiles("sorted", 2, [P, PASSES1 * DUOS], F32)
        cash1_two = tiles("cash1_", PAIRS // 2, [P, 4 * M], BF16)
        cash1_t = [cash1_two[n // 2][:, 2 * M * (n % 2) : 2 * M * (n % 2 + 1)] for n in range(PAIRS)]
        cash2_t = tiles("cash2_", PAIRS, [P, 2 * R], BF16)
        a_t = tiles("a", Z, [P, PASSES1, 2 * M], U8)
        b_t = tiles("b", Z, [P, 2 * R], U8)
        a_sc_first = sb.tile([P, PASSES1, M], U8, align_bytes=64)
        a_sc_rest = sb.tile([P, PASSES1 * (Z - 1), M], U8, align_bytes=64)
        a_sc = [a_sc_first[:, g, :] for g in range(PASSES1)] + [a_sc_rest[:, g, :] for g in range(PASSES1 * (Z - 1))]
        b_sc = sb.tile([P, Z, R], U8, align_bytes=64)
        owed_rows = sb.tile([P, M], BF16)
        owed_t = sb.tile([P, 2 * Z, 4], BF16)

        stage = tiles("stage", 3, [P, 2 * PASSES1 * DUOS], F32)
        pay_codes = tiles("pay_codes", 2, [P, 2 * PASSES1 * P], U32)
        pay_sc = tiles("pay_sc", 2, [P, 2 * PASSES1 * P], U8)
        paid_codes = tiles("paid_codes", 2, [P, PAIR], U32)
        paid_sc = tiles("paid_sc", 2, [P, PAIR], U8)
        have1 = tiles("have1_", 4, [P, M], BF16)
        paid_t = tiles("paid", 2, [P, 2 * R], F32)
        in2_sb = tiles("in2_sb", 2, [P, 2 * R], F32)

        pay_ps = [ps.tile([P, BANK], F32, name="pay_ps%d" % j) for j in range(2)]
        in1_ps = [ps.tile([P, BANK], F32, name="in1_ps%d" % j) for j in range(2)]
        in2_ps = [ps.tile([P, BANK], F32, name="in2_ps%d" % j) for j in range(2)]
        have_ps = ps.tile([P, BANK], F32)
        owed2_ps = ps.tile([P, BANK], F32)
        owed2_row = owed2_ps[:, 0:DUOS].bitcast(BF16)

        def live(n):
            return 0 <= n < PAIRS

        def load_pay_columns(n, j, k0, k1):
            nc.sync.dma_start(out=pay_t[n][:, N * j + k0 : N * j + k1], in_=rows(pay, n)[:, j, k0:k1])

        def load_pair(dst, tensor, n):
            nc.sync.dma_start(out=dst[n][:].rearrange("p (j k) -> p j k", j=2), in_=rows(tensor, n))

        def load_cash1_two_pairs(n):
            z, q = divmod(n, PAIRS_PER_ZONE)
            nc.sync.dma_start(
                out=cash1_two[n // 2][:].rearrange("p (h k) -> p h k", h=2),
                in_=cash1[z, q * PAIR : (q + 2) * PAIR, :].rearrange("(h p j) k -> p h (j k)", h=2, j=2),
            )

        def load_scales(plane, scales, g0, g1):
            for q in range(4):
                nc.sync.dma_start(
                    out=plane[32 * q : 32 * q + 4, :, :].bitcast(I32),
                    in_=scales.bitcast(I32)[g0:g1, 4 * q : 4 * q + 4, :].rearrange("g r n -> r g n"),
                )

        def load_a(z):
            nc.sync.dma_start(
                out=a_t[z][:].bitcast(I32),
                in_=a_words.bitcast(I32)[PASSES1 * z : PASSES1 * (z + 1), :, :].rearrange("g p n -> p g n"),
            )

        def load_b(z):
            nc.sync.dma_start(out=b_t[z][:].bitcast(I32), in_=b_words.bitcast(I32)[z, :, :])

        def loads_for_step(w):
            if live(w + 2) and (w + 2) % PAIRS_PER_ZONE == 0:
                load_a((w + 2) // PAIRS_PER_ZONE)
            if live(w + 2) and w % 2 == 0:
                load_cash1_two_pairs(w + 2)
            if live(w) and w % PAIRS_PER_ZONE == 0:
                load_b(w // PAIRS_PER_ZONE)
            if live(w - 1):
                load_pair(cash2_t, cash2, w - 1)
            if w + 2 == PAIRS_PER_ZONE:
                load_scales(a_sc_rest, a_scales, PASSES1, PASSES1 * Z)
            if live(w + 4):
                load_pair(pay_t, pay, w + 4)

        def pay_duos(n, j):
            return pay_t[n][:, N * j : N * (j + 1)].bitcast(F32)

        def every_second_duo(n, j, g, u):
            return pay_duos(n, j)[:, DUOS * g + u : DUOS * (g + 1) : 2]

        def is_sorted(n, j):
            return n > 0 and (n < HEAD_PAIRS or j == 1)

        def sort_pay(n, j):
            nc.scalar.copy(
                out=sorted_t[j][:].rearrange("s (u c i) -> s c u i", u=2, i=4),
                in_=pay_duos(n, j).rearrange("s (c i u) -> s c u i", u=2, i=4),
            )

        def transpose_pay(n, j, bank):
            for g in range(PASSES1):
                for u in range(2):
                    if is_sorted(n, j):
                        duos = sorted_t[j][:, DUOS * u + P * g : DUOS * u + P * (g + 1)]
                    else:
                        duos = every_second_duo(n, j, g, u)
                    c = (2 * g + u) * P
                    nc.tensor.transpose(pay_ps[bank][:, c : c + P], duos, ident[:])

        def copy_turned_pay(n, j, bank):
            nc.scalar.copy(
                out=stage[n % 3][:, BANK * j : BANK * (j + 1)].rearrange("p (g s u) -> p g s u", g=PASSES1, u=2),
                in_=pay_ps[bank][:].rearrange("p (g u s) -> p g s u", g=PASSES1, u=2),
            )

        def turn_pay(n, j):
            transpose_pay(n, j, bank=j)
            copy_turned_pay(n, j, bank=j)

        def quantize_pay(n, first, count):
            cols = slice(first * P, (first + count) * P)
            nc.vector.quantize_mx(
                out=pay_codes[n % 2][:, cols].bitcast(FP8X4),
                scales=pay_sc[n % 2][:, cols],
                in_=stage[n % 3][:, first * DUOS : (first + count) * DUOS].bitcast(BF16),
            )

        def quantize_pay_tile(n, j):
            quantize_pay(n, PASSES1 * j, PASSES1)

        def matmul1(n, j):
            z = n // PAIRS_PER_ZONE
            for g in range(PASSES1):
                cols = slice((PASSES1 * j + g) * P, (PASSES1 * j + g + 1) * P)
                nc.tensor.matmul_mx(
                    out=in1_ps[j][:],
                    lhsT=pay_codes[n % 2][:, cols].bitcast(FP8X4),
                    lhsT_scale=pay_sc[n % 2][:, cols],
                    rhs=a_t[z][:, g, :].bitcast(FP4X4),
                    rhs_scale=a_sc[PASSES1 * z + g],
                    start=(g == 0),
                    stop=(g == PASSES1 - 1),
                )

        def add_cash1(n, j):
            nc.vector.tensor_tensor(
                out=have1[2 * (n % 2) + j][:].rearrange("s (u p e) -> s u p e", u=2, e=2),
                in0=in1_ps[j][:].rearrange("s (p u e) -> s u p e", u=2, e=2),
                in1=cash1_t[n][:, M * j : M * (j + 1)].rearrange("s (p u e) -> s u p e", u=2, e=2),
                op=ADD,
            )

        def transpose_have(n):
            for j in range(2):
                duos = have1[2 * (n % 2) + j][:].bitcast(F32)
                for u in range(2):
                    c = (2 * u + j) * P
                    nc.tensor.transpose(have_ps[:, c : c + P], duos[:, u * P : (u + 1) * P], ident[:])

        def paid1(n):
            return paid_t[n % 2][:, 0:R].bitcast(BF16)

        def min_owed1(n):
            z = n // PAIRS_PER_ZONE
            nc.vector.tensor_tensor(
                out=paid1(n).rearrange("p (s u e) -> p s u e", u=2, e=2),
                in0=have_ps[:].bitcast(BF16).rearrange("p (u s e) -> p s u e", u=2, e=2),
                in1=owed_t[:, z, :].rearrange("p (u e) -> p u e", e=2).unsqueeze(1).to_broadcast([P, PAIR, 2, 2]),
                op=MIN,
            )

        def quantize_paid(n):
            nc.vector.quantize_mx(out=paid_codes[n % 2][:].bitcast(FP8X4), scales=paid_sc[n % 2][:], in_=paid1(n))

        def matmul2(n, j):
            z = n // PAIRS_PER_ZONE
            cols = slice(j * P, (j + 1) * P)
            nc.tensor.matmul_mx(
                out=in2_ps[j][:],
                lhsT=paid_codes[n % 2][:, cols].bitcast(FP8X4),
                lhsT_scale=paid_sc[n % 2][:, cols],
                rhs=b_t[z][:].bitcast(FP4X4),
                rhs_scale=b_sc[:, z, :],
                start=True,
                stop=True,
            )

        def copy_in2(n, j):
            nc.scalar.copy(out=in2_sb[n % 2][:, R * j : R * (j + 1)], in_=in2_ps[j][:])

        def sums(n):
            return stage[n % 3] if live(n + 3) else paid_t[(n + 1) % 2]

        def add_cash2_gpsimd(n):
            nc.gpsimd.tensor_tensor(out=sums(n)[:], in0=in2_sb[n % 2][:], in1=cash2_t[n][:], op=ADD)

        def add_cash2_vector(n, j):
            cols = slice(R * j, R * (j + 1))
            nc.vector.tensor_tensor(out=in2_sb[n % 2][:, cols], in0=in2_ps[j][:], in1=cash2_t[n][:, cols], op=ADD)

        def turn_owed():
            duos = owed_rows[:].bitcast(F32)
            for u in range(2):
                nc.tensor.transpose(owed2_ps[:, u * P : (u + 1) * P], duos[:, u:DUOS:2], ident[:])
            nc.scalar.copy(
                out=owed_t[:].bitcast(F32),
                in_=owed2_ps[:, 0 : 2 * P].rearrange("p (u i) -> p i u", u=2)[:, 0 : 2 * Z, :],
            )

        def spread_owed2(z):
            duos = owed_t[:, Z + z, :].bitcast(F32)
            for u in range(2):
                nc.tensor.transpose(owed2_ps[:, u:DUOS:2], duos[:, u : u + 1].to_broadcast([P, P]), ident[:])

        def finish_pair(n):
            result = pay_t[n][:].bitcast(F32).rearrange("s (j r) -> s j r", j=2)
            nc.vector.tensor_tensor(
                out=result,
                in0=sums(n)[:].rearrange("s (j r) -> s j r", j=2),
                in1=owed2_row.unsqueeze(1).to_broadcast([P, 2, R]),
                op=MIN,
            )
            nc.sync.dma_start(out=rows(out, n), in_=result)

        def finish_columns(n, j, total, r0, r1):
            cols = slice(R * j + r0, R * j + r1)
            result = pay_t[n][:].bitcast(F32)[:, cols]
            nc.vector.tensor_tensor(out=result, in0=total[:, cols], in1=owed2_row[:, r0:r1], op=MIN)
            nc.sync.dma_start(out=rows(out, n)[:, j, r0:r1], in_=result)

        def zero(plane):
            nc.vector.memset(plane[:].rearrange("p g n -> p (g n)").bitcast(I32), 0)

        zero(a_sc_first)
        make_identity(nc, ident[:])
        nc.vector.memset(owed_rows[:].bitcast(F32), 0.0)
        zero(b_sc)
        zero(a_sc_rest)

        for g in range(PASSES1):
            load_pay_columns(0, 0, K_PASS * g, K_PASS * (g + 1))
        load_pay_columns(0, 1, 0, N)
        load_scales(a_sc_first, a_scales, 0, PASSES1)
        load_a(0)
        for j in range(2):
            load_pay_columns(1, j, 0, N)
        load_pair(cash1_t, cash1, 0)
        load_pair(pay_t, pay, 2)
        load_pair(cash1_t, cash1, 1)
        nc.sync.dma_start(out=owed_rows[0:Z, :], in_=owed1)
        nc.sync.dma_start(out=owed_rows[Z : 2 * Z, :], in_=owed2)
        load_pair(pay_t, pay, 3)
        load_scales(b_sc, b_scales, 0, Z)
        load_b(0)
        load_pair(pay_t, pay, 4)
        load_cash1_two_pairs(2)
        for w in range(1, 1 + LEAD):
            loads_for_step(w)

        for g in range(PASSES1):
            for u in range(2):
                nc.tensor.transpose(pay_ps[g][:, u * P : (u + 1) * P], every_second_duo(0, 0, g, u), ident[:])
            nc.scalar.copy(
                out=stage[0][:, DUOS * g : DUOS * (g + 1)].rearrange("p (s u) -> p s u", u=2),
                in_=pay_ps[g][:, 0 : 2 * P].rearrange("p (u s) -> p s u", u=2),
            )
            quantize_pay(0, g, 1)
        transpose_pay(0, 1, bank=0)
        copy_turned_pay(0, 1, bank=0)
        quantize_pay_tile(0, 1)
        sort_pay(1, 0)
        sort_pay(1, 1)

        matmul1(0, 0)
        add_cash1(0, 0)
        turn_pay(1, 0)

        matmul1(0, 1)
        quantize_pay_tile(1, 0)
        add_cash1(0, 1)
        sort_pay(2, 0)
        turn_pay(1, 1)
        turn_owed()
        sort_pay(2, 1)

        matmul1(1, 0)
        quantize_pay_tile(1, 1)
        transpose_have(0)
        add_cash1(1, 0)
        min_owed1(0)
        turn_pay(2, 0)
        sort_pay(3, 0)

        matmul1(1, 1)
        quantize_pay_tile(2, 0)
        quantize_paid(0)
        add_cash1(1, 1)
        turn_pay(2, 1)
        sort_pay(3, 1)

        matmul1(2, 0)
        quantize_pay_tile(2, 1)
        turn_pay(3, 0)
        transpose_have(1)
        min_owed1(1)
        turn_pay(3, 1)
        add_cash1(2, 0)

        for j in range(2):
            matmul2(0, j)
        matmul1(2, 1)
        for j in range(2):
            copy_in2(0, j)
        sort_pay(4, 1)
        transpose_pay(4, 0, bank=0)

        for w in range(1, PAIRS):
            loads_for_step(w + LEAD)
            if live(w + 2):
                quantize_pay(w + 2, 0, 2 * PASSES1)
            quantize_paid(w)
            add_cash2_gpsimd(w - 1)
            if live(w + 3):
                copy_turned_pay(w + 3, 0, bank=0)
            if live(w + 2):
                matmul1(w + 2, 0)
            matmul2(w, 0)
            if live(w + 1):
                add_cash1(w + 1, 1)
            if w < LAST:
                copy_in2(w, 0)
            if live(w + 3):
                turn_pay(w + 3, 1)
            if live(w + 1):
                transpose_have(w + 1)
            if live(w - 2):
                finish_pair(w - 2)
            if live(w + 2):
                add_cash1(w + 2, 0)
            if live(w + 1):
                min_owed1(w + 1)
            matmul2(w, 1)
            if live(w + 2):
                matmul1(w + 2, 1)
            if w < LAST:
                copy_in2(w, 1)
            if live(w + 4):
                sort_pay(w + 4, 1)
                transpose_pay(w + 4, 0, bank=0)
            if (w - 1) % PAIRS_PER_ZONE == 0:
                spread_owed2((w - 1) // PAIRS_PER_ZONE)

        for j in range(2):
            add_cash2_vector(LAST, j)
        for j in range(2):
            finish_columns(LAST, j, in2_sb[LAST % 2], 0, R)
        finish_columns(LAST - 1, 0, sums(LAST - 1), 0, R)
        for half in range(2):
            finish_columns(LAST - 1, 1, sums(LAST - 1), half * R // 2, (half + 1) * R // 2)
